import numpy as np
import ml_dtypes


def mxq(x, axis, fmt="e4m3"):
    dtype, down = {"e4m3": (ml_dtypes.float8_e4m3fn, 7), "e5m2": (ml_dtypes.float8_e5m2, 14)}[fmt]
    v = np.moveaxis(np.asarray(x, np.float32).astype(ml_dtypes.bfloat16).astype(np.float64), axis, -1)
    blocks = v.reshape(v.shape[:-1] + (-1, 32))
    amax = np.abs(blocks).max(-1, keepdims=True)
    byte = np.maximum(np.where(amax > 0, np.frexp(amax)[1] - 1 + 127, 0) - down, 1)
    scale = np.exp2(byte - 127.0)
    codes = (blocks / scale).astype(np.float32).astype(dtype).astype(np.float64)
    return np.moveaxis((codes * scale).reshape(v.shape), -1, axis)


WIDE = False


def mx_kscale(k):
    if not WIDE:
        return np.ones(k)
    levels = np.array([10, -10, 5, -5, 0])
    if k % 512:
        return np.exp2(np.random.permutation(np.resize(levels, k // 32))).repeat(32)
    a = np.empty((k // 512, 16))
    for p in range(k // 512):
        a[p, :8] = np.random.permutation(np.resize(levels, 8))
        for g in range(8):
            far = levels[np.abs(levels - a[p, g]) >= 10]
            a[p, g + 8] = far[np.random.randint(len(far))]
    return np.exp2(a.ravel()).repeat(32)


def f64(x):
    return np.asarray(x).astype(np.float64)


def striped(idx):
    return np.tile(np.asarray(idx).reshape(-1, 16).T, (8, 1)).astype(np.uint16)


def unstriped(offs):
    return offs[:16].T.reshape(-1).astype(np.int64)


E2M1 = np.array([0.0, 0.5, 1.0, 1.5, 2.0, 3.0, 4.0, 6.0, -0.0, -0.5, -1.0, -1.5, -2.0, -3.0, -4.0, -6.0])


def pack_weight(w, fmt):
    k, n = w.shape
    w = f64(np.asarray(w, np.float32).astype(ml_dtypes.bfloat16)).reshape(k // 32, 32, n)
    amax = np.abs(w).max(1)
    if fmt == "e4m3":
        byte = np.frexp(amax)[1] - 1 + 127 - 7
    else:
        mant, ex = np.frexp(amax / 6.0)
        byte = np.where(mant > 0.5, ex, ex - 1) + 127
    byte = np.clip(np.where(amax > 0, byte, 1), 1, 254)
    scaled = (w * np.exp2(127.0 - byte)[:, None, :]).reshape(k, n).astype(np.float32)
    by_word = np.ascontiguousarray(scaled.reshape(k // 512, 128, 4, n).transpose(0, 1, 3, 2))
    if fmt == "e4m3":
        words = by_word.astype(ml_dtypes.float8_e4m3fn).view(np.uint8)
    else:
        c = by_word.astype(ml_dtypes.float4_e2m1fn).view(np.uint8) & 0xF
        words = (c[..., 0::2] | (c[..., 1::2] << 4)).reshape(k // 512, 128, 2 * n)
    return np.ascontiguousarray(words), np.ascontiguousarray(byte.astype(np.uint8).reshape(k // 512, 16, n))


def unpack_weight(words, scales, fmt):
    g, _, n = scales.shape
    words = np.ascontiguousarray(words).reshape(g, 128, n, -1)
    if fmt == "e4m3":
        vals = words.view(ml_dtypes.float8_e4m3fn).astype(np.float64)
    else:
        nib = np.empty((g, 128, n, 4), np.uint8)
        nib[..., 0::2] = words & 0xF
        nib[..., 1::2] = words >> 4
        vals = E2M1[nib]
    vals = vals * np.repeat(np.exp2(scales.astype(np.float64) - 127.0), 8, axis=1)[..., None]
    return vals.transpose(0, 1, 3, 2).reshape(g * 512, n)


D, T, I, Q, E = 512, 2048, 512, 128, 512


def setup_inputs():
    n = np.random.standard_normal
    idx = np.random.permutation(T)[:I]
    fd = mx_kscale(D)
    fi = mx_kscale(I)
    ti = np.ones(T)
    ti[idx] = fi
    keysp = pack_weight(n((D, T)) / fd[:, None], "e4m3")
    return {
        "query": (n((D, Q)) * 0.25 / np.sqrt(D) * fd[:, None]).astype(np.float32),
        "keys_words": keysp[0],
        "keys_scales": keysp[1],
        "sharp": np.tile(np.random.uniform(0.3, 2.5, T), (128, 1)).astype(np.float32),
        "tbias": np.tile(0.4 * n(T), (128, 1)).astype(np.float32),
        "size": (np.random.uniform(0.5, 2.0, (1, I)) * fi).astype(np.float32),
        "vals": (n((E, T)) / ti).astype(np.float32),
        "offs": striped(idx),
    }


def reference(query, keys_words, keys_scales, sharp, tbias, size, vals, offs):
    idx = unstriped(offs)
    keysu = unpack_weight(keys_words, keys_scales, "e4m3")
    queryq = mxq(f64(query), 0, "e4m3")
    keysidxg = keysu[:, idx]
    a = queryq.T @ keysidxg
    s = a * f64(sharp)[:1][:, idx] + f64(tbias)[:1][:, idx]
    p = np.exp(s - np.max(s, axis=1, keepdims=True))
    w = p * f64(size) / np.sum(p, axis=1, keepdims=True)
    wt = w.T
    vt = f64(vals)[:, idx].T
    wtq = mxq(wt, 0, "e4m3")
    vtq = mxq(vt, 0, "e4m3")
    o = wtq.T @ vtq
    return o

@@ -1,0 +1,194 @@
+from contextlib import ExitStack
+
+import concourse.mybir as mybir
+
+D, T, I, Q, E = 512, 2048, 512, 128, 512
+FLOPS = 2 * Q * I * (D + E)
+
+F32 = mybir.dt.float32
+BF16 = mybir.dt.bfloat16
+I32 = mybir.dt.int32
+U32 = mybir.dt.uint32
+U16 = mybir.dt.uint16
+U8 = mybir.dt.uint8
+FP8X4 = mybir.dt.float8_e4m3fn_x4
+ALU = mybir.AluOpType
+ACT = mybir.ActivationFunctionType
+
+P = 128
+PACK = 4
+SHARP_ROW = 8
+BIAS_ROW = 72
+
+
+def tile_attend_tokensharpness_kernel(tc, query, keys_words, keys_scales, sharp, tbias, size, vals, offs, out):
+    nc = tc.nc
+    with ExitStack() as ctx:
+        sb = ctx.enter_context(tc.tile_pool(name="sb", bufs=1))
+        ps = ctx.enter_context(tc.psum_pool(name="ps", bufs=1))
+
+        def sbuf(name, shape, dtype, tag=None):
+            return sb.tile(shape, dtype, align_bytes=64, name=name, tag=tag or name)
+
+        def turn(pairs, bank_tag, name):
+            words = pairs[:].bitcast(F32)
+            turned = ps.tile([P, 2, P], F32, tag=bank_tag, name=name + "_turned")
+            for u in range(2):
+                nc.tensor.transpose(turned[:, u, :], words[:, u::2], ident[:])
+            grouped = sbuf(name + "_grouped", [P, P * PACK], BF16)
+            nc.scalar.copy(
+                out=grouped[:].bitcast(F32).rearrange("p (c u) -> p c u", u=2),
+                in_=turned[:].rearrange("p u c -> p c u"),
+            )
+            return grouped
+
+        def quantize(grouped, name, tag=None):
+            codes = sbuf(name + "_codes", [P, P], U32, tag)
+            scales = sbuf(name + "_scales", [P, P], U8)
+            nc.vector.quantize_mx(out=codes[:].bitcast(FP8X4), scales=scales[:], in_=grouped[:])
+            return codes, scales
+
+        def load_vals(j, tag):
+            pool = sbuf(f"val_pool{j}", [P, T], F32, tag)
+            nc.sync.dma_start(out=pool[:], in_=vals[j * P : (j + 1) * P, :])
+            return pool
+
+        def gather_vals(j, pool, tag=None):
+            listed = sbuf(f"listed_vals{j}", [P, I], BF16, tag)
+            nc.vector.tensor_copy(listed[:], pool[:].indirect(offsets[:]))
+            return turn(listed, f"vals{j % 2}", f"v{j}")
+
+        def listed_columns(pool, row, name, tag):
+            listed = sbuf(name + "_listed", [P, I], F32, tag)
+            nc.vector.tensor_copy(listed[:], pool[:].indirect(offsets[:]))
+            turned = ps.tile([P, I // P, P], F32, tag=name, name=name + "_turned")
+            for r in range(I // P):
+                nc.tensor.transpose(turned[:, r, :], listed[:, r * P : (r + 1) * P], ident[:])
+            cols = sbuf(name + "_cols", [P, I // P], F32)
+            nc.scalar.activation(out=cols[:], in_=turned[:, :, row], func=ACT.Copy)
+            return cols
+
+        offsets = sb.tile([P, I // 16], U16)
+        nc.sync.dma_start(offsets[:], offs)
+        q_raw = sbuf("q_raw", [P, PACK, Q], F32)
+        nc.sync.dma_start(out=q_raw[:], in_=query.rearrange("(p j) q -> p j q", j=PACK))
+        key_pool = sbuf("key_pool", [P, T], U32)
+        nc.sync.dma_start(
+            out=key_pool[:].bitcast(I32), in_=keys_words[0].rearrange("p n t -> p (n t)").bitcast(I32)
+        )
+
+        scale_pool = sbuf("scale_pool", [P, T], U8)
+        nc.vector.memset(scale_pool[:].bitcast(I32), 0)
+        for quad in range(4):
+            nc.scalar.dma_start(
+                out=scale_pool[32 * quad : 32 * quad + 4, :].bitcast(I32),
+                in_=keys_scales[0, 4 * quad : 4 * quad + 4, :].bitcast(I32),
+            )
+        ones = sbuf("ones", [P, P], F32)
+        nc.vector.memset(ones[:], 1.0)
+        ident = sbuf("ident", [P, P], F32)
+        nc.gpsimd.affine_select(
+            out=ident[:],
+            in_=ones[:],
+            pattern=[[-1, P]],
+            compare_op=ALU.is_equal,
+            fill=0.0,
+            base=0,
+            channel_multiplier=1,
+        )
+        val_pool0 = load_vals(0, "ones")
+        sharp_pool = sbuf("sharp_pool", [P, T], F32)
+        nc.vector.memset(sharp_pool[:].bitcast(I32), 0)
+        nc.scalar.dma_start(out=sharp_pool[SHARP_ROW : SHARP_ROW + 1, :], in_=sharp[0:1, :])
+        bias_pool = sbuf("bias_pool", [P, T], F32)
+        nc.vector.memset(bias_pool[:].bitcast(I32), 0)
+        nc.scalar.dma_start(out=bias_pool[BIAS_ROW : BIAS_ROW + 1, :], in_=tbias[0:1, :])
+
+        q_grouped = sbuf("q_grouped", [P, Q * PACK], BF16)
+        nc.scalar.copy(
+            out=q_grouped[:].rearrange("p (q j) -> p q j", j=PACK), in_=q_raw[:].rearrange("p j q -> p q j")
+        )
+        val_pool1 = load_vals(1, "q_raw")
+        q_codes, q_scales = quantize(q_grouped, "q")
+        val_pool2 = load_vals(2, "q_grouped")
+
+        key_scales = sbuf("key_scales", [P, I], U8)
+        nc.vector.tensor_copy(key_scales[:], scale_pool[:].indirect(offsets[:]))
+        size_cols = sbuf("size_cols", [P, PACK], F32, "scale_pool")
+        nc.sync.dma_start(out=size_cols[:], in_=size[0].rearrange("(p t) -> p t", t=PACK))
+        sharp_cols = listed_columns(sharp_pool, SHARP_ROW, "sharp", None)
+        key_codes = sbuf("key_codes", [P, I], U32, "sharp_pool")
+        nc.vector.tensor_copy(key_codes[:], key_pool[:].indirect(offsets[:]))
+        bias_cols = listed_columns(bias_pool, BIAS_ROW, "bias", "key_pool")
+        val_pool3 = load_vals(3, "sharp_listed")
+
+        size_rows = ps.tile([P, PACK, P], F32, tag="size")
+        for t in range(PACK):
+            nc.tensor.transpose(size_rows[:, t, :], size_cols[:, t : t + 1].to_broadcast([P, P]), ident[:])
+
+        raw_scores = ps.tile([P, I // P, Q], F32, tag="raw")
+        for r in range(I // P):
+            slots = slice(r * P, (r + 1) * P)
+            nc.tensor.matmul_mx(
+                out=raw_scores[:, r, :],
+                lhsT=key_codes[:, slots].bitcast(FP8X4),
+                lhsT_scale=key_scales[:, slots],
+                rhs=q_codes[:].bitcast(FP8X4),
+                rhs_scale=q_scales[:],
+                start=True,
+                stop=True,
+            )
+        scores_t = sbuf("scores_t", [P, I // P, Q], F32)
+        scores = ps.tile([P, I], F32, tag="scores")
+        for r in range(I // P):
+            nc.scalar.activation(
+                out=scores_t[:, r, :],
+                in_=raw_scores[:, r, :],
+                func=ACT.Identity,
+                scale=sharp_cols[:, r : r + 1],
+                bias=bias_cols[:, r : r + 1],
+            )
+            nc.tensor.transpose(scores[:, r * P : (r + 1) * P], scores_t[:, r, :], ident[:])
+
+        v_grouped = [gather_vals(0, val_pool0, "bias_pool"), gather_vals(1, val_pool1)]
+
+        neg_max = sbuf("neg_max", [P, 1], F32, "q_raw")
+        nc.vector.tensor_reduce(out=neg_max[:], in_=scores[:], axis=mybir.AxisListType.X, op=ALU.max, negate=True)
+        probs = sbuf("probs", [P, I], F32)
+        row_sum = sbuf("row_sum", [P, 1], F32)
+        nc.scalar.activation(out=probs[:], in_=scores[:], func=ACT.Exp, bias=neg_max[:], accum_out=row_sum[:])
+        v_grouped.append(gather_vals(2, val_pool2))
+        inv_sum = sbuf("inv_sum", [P, 1], F32, "q_grouped")
+        nc.vector.reciprocal(inv_sum[:], row_sum[:])
+        weights = sbuf("weights", [P, I], BF16)
+        nc.vector.scalar_tensor_tensor(
+            out=weights[:].rearrange("q (s t) -> q s t", t=PACK),
+            in0=probs[:].rearrange("q (s t) -> q s t", t=PACK),
+            scalar=inv_sum[:],
+            in1=size_rows[:].rearrange("q t s -> q s t"),
+            op0=ALU.mult,
+            op1=ALU.mult,
+        )
+        w_grouped = turn(weights, "raw", "w")
+        v_grouped.append(gather_vals(3, val_pool3))
+        w_codes, w_scales = quantize(w_grouped, "w", "sharp_listed")
+
+        def product(blocks, bank_tag, copy):
+            acc = ps.tile([P, len(blocks), P], F32, tag=bank_tag, name=f"acc{blocks[0]}")
+            for n, j in enumerate(blocks):
+                v_codes, v_scales = quantize(v_grouped[j], f"v{j}")
+                nc.tensor.matmul_mx(
+                    out=acc[:, n, :],
+                    lhsT=w_codes[:].bitcast(FP8X4),
+                    lhsT_scale=w_scales[:],
+                    rhs=v_codes[:].bitcast(FP8X4),
+                    rhs_scale=v_scales[:],
+                    start=True,
+                    stop=True,
+                )
+            result = sbuf(f"result{blocks[0]}", [P, len(blocks) * P], F32)
+            copy(out=result[:], in_=acc[:].rearrange("q n e -> q (n e)"))
+            nc.sync.dma_start(out=out[:, blocks[0] * P : (blocks[-1] + 1) * P], in_=result[:])
+
+        product([0, 1, 2], "sharp", nc.scalar.copy)
+        product([3], "bias", nc.vector.tensor_copy)

@@ -1,6 +1,7 @@
 from contextlib import ExitStack
 
 import concourse.mybir as mybir
+from concourse.masks import make_identity
 
 D, T, I, Q, E = 512, 2048, 512, 128, 512
 FLOPS = 2 * Q * I * (D + E)
@@ -30,37 +31,31 @@ def tile_attend_tokensharpness_kernel(tc, query, keys_words, keys_scales, sharp,
         def sbuf(name, shape, dtype, tag=None):
             return sb.tile(shape, dtype, align_bytes=64, name=name, tag=tag or name)
 
-        def turn(pairs, bank_tag, name):
+        def turn(pairs, grouped, bank_tag, name):
             words = pairs[:].bitcast(F32)
             turned = ps.tile([P, 2, P], F32, tag=bank_tag, name=name + "_turned")
             for u in range(2):
                 nc.tensor.transpose(turned[:, u, :], words[:, u::2], ident[:])
-            grouped = sbuf(name + "_grouped", [P, P * PACK], BF16)
             nc.scalar.copy(
-                out=grouped[:].bitcast(F32).rearrange("p (c u) -> p c u", u=2),
+                out=grouped.bitcast(F32).rearrange("p (c u) -> p c u", u=2),
                 in_=turned[:].rearrange("p u c -> p c u"),
             )
-            return grouped
 
         def quantize(grouped, name, tag=None):
-            codes = sbuf(name + "_codes", [P, P], U32, tag)
-            scales = sbuf(name + "_scales", [P, P], U8)
+            cols = grouped.shape[1] // PACK
+            codes = sbuf(name + "_codes", [P, cols], U32, tag)
+            scales = sbuf(name + "_scales", [P, cols], U8)
             nc.vector.quantize_mx(out=codes[:].bitcast(FP8X4), scales=scales[:], in_=grouped[:])
             return codes, scales
 
-        def load_vals(j, tag):
-            pool = sbuf(f"val_pool{j}", [P, T], F32, tag)
-            nc.sync.dma_start(out=pool[:], in_=vals[j * P : (j + 1) * P, :])
-            return pool
-
-        def gather_vals(j, pool, tag=None):
+        def gather_vals(j, grouped, bank_tag, tag=None):
             listed = sbuf(f"listed_vals{j}", [P, I], BF16, tag)
-            nc.vector.tensor_copy(listed[:], pool[:].indirect(offsets[:]))
-            return turn(listed, f"vals{j % 2}", f"v{j}")
+            nc.vector.tensor_copy(listed[:], val_pools[j][:].indirect(offsets[:]))
+            turn(listed, grouped, bank_tag, f"v{j}")
 
         def listed_columns(pool, row, name, tag):
             listed = sbuf(name + "_listed", [P, I], F32, tag)
-            nc.vector.tensor_copy(listed[:], pool[:].indirect(offsets[:]))
+            nc.vector.tensor_copy(listed[:], pool[:, :T].indirect(offsets[:]))
             turned = ps.tile([P, I // P, P], F32, tag=name, name=name + "_turned")
             for r in range(I // P):
                 nc.tensor.transpose(turned[:, r, :], listed[:, r * P : (r + 1) * P], ident[:])
@@ -72,55 +67,50 @@ def tile_attend_tokensharpness_kernel(tc, query, keys_words, keys_scales, sharp,
         nc.sync.dma_start(offsets[:], offs)
         q_raw = sbuf("q_raw", [P, PACK, Q], F32)
         nc.sync.dma_start(out=q_raw[:], in_=query.rearrange("(p j) q -> p j q", j=PACK))
+        size_cols = sbuf("size_cols", [P, PACK], F32)
+        nc.sync.dma_start(out=size_cols[:], in_=size[0].rearrange("(p t) -> p t", t=PACK))
+        scale_pool = sbuf("scale_pool", [P, T + 4], U8)
+        nc.vector.memset(scale_pool[:].bitcast(I32), 0)
+        for quad in range(4):
+            nc.sync.dma_start(
+                out=scale_pool[32 * quad : 32 * quad + 4, :T].bitcast(I32),
+                in_=keys_scales[0, 4 * quad : 4 * quad + 4, :].bitcast(I32),
+            )
         key_pool = sbuf("key_pool", [P, T], U32)
         nc.sync.dma_start(
             out=key_pool[:].bitcast(I32), in_=keys_words[0].rearrange("p n t -> p (n t)").bitcast(I32)
         )
-
-        scale_pool = sbuf("scale_pool", [P, T], U8)
-        nc.vector.memset(scale_pool[:].bitcast(I32), 0)
-        for quad in range(4):
-            nc.scalar.dma_start(
-                out=scale_pool[32 * quad : 32 * quad + 4, :].bitcast(I32),
-                in_=keys_scales[0, 4 * quad : 4 * quad + 4, :].bitcast(I32),
-            )
-        ones = sbuf("ones", [P, P], F32)
-        nc.vector.memset(ones[:], 1.0)
-        ident = sbuf("ident", [P, P], F32)
-        nc.gpsimd.affine_select(
-            out=ident[:],
-            in_=ones[:],
-            pattern=[[-1, P]],
-            compare_op=ALU.is_equal,
-            fill=0.0,
-            base=0,
-            channel_multiplier=1,
-        )
-        val_pool0 = load_vals(0, "ones")
-        sharp_pool = sbuf("sharp_pool", [P, T], F32)
+        sharp_pool = sbuf("sharp_pool", [P, T + 1], F32)
         nc.vector.memset(sharp_pool[:].bitcast(I32), 0)
-        nc.scalar.dma_start(out=sharp_pool[SHARP_ROW : SHARP_ROW + 1, :], in_=sharp[0:1, :])
+        nc.sync.dma_start(out=sharp_pool[SHARP_ROW : SHARP_ROW + 1, :T], in_=sharp[0:1, :])
         bias_pool = sbuf("bias_pool", [P, T], F32)
-        nc.vector.memset(bias_pool[:].bitcast(I32), 0)
-        nc.scalar.dma_start(out=bias_pool[BIAS_ROW : BIAS_ROW + 1, :], in_=tbias[0:1, :])
+        nc.gpsimd.memset(bias_pool[:].bitcast(I32), 0)
+        nc.sync.dma_start(out=bias_pool[BIAS_ROW : BIAS_ROW + 1, :], in_=tbias[0:1, :])
+        ident = sbuf("ident", [P, P], F32)
+        make_identity(nc, ident[:])
+        val_pools = []
+
+        def load_vals(tag):
+            j = len(val_pools)
+            val_pool = sbuf(f"val_pool{j}", [P, T], F32, tag)
+            nc.sync.dma_start(out=val_pool[:], in_=vals[j * P : (j + 1) * P, :])
+            val_pools.append(val_pool)
 
         q_grouped = sbuf("q_grouped", [P, Q * PACK], BF16)
         nc.scalar.copy(
             out=q_grouped[:].rearrange("p (q j) -> p q j", j=PACK), in_=q_raw[:].rearrange("p j q -> p q j")
         )
-        val_pool1 = load_vals(1, "q_raw")
-        q_codes, q_scales = quantize(q_grouped, "q")
-        val_pool2 = load_vals(2, "q_grouped")
-
+        load_vals("q_raw")
         key_scales = sbuf("key_scales", [P, I], U8)
-        nc.vector.tensor_copy(key_scales[:], scale_pool[:].indirect(offsets[:]))
-        size_cols = sbuf("size_cols", [P, PACK], F32, "scale_pool")
-        nc.sync.dma_start(out=size_cols[:], in_=size[0].rearrange("(p t) -> p t", t=PACK))
-        sharp_cols = listed_columns(sharp_pool, SHARP_ROW, "sharp", None)
-        key_codes = sbuf("key_codes", [P, I], U32, "sharp_pool")
+        nc.vector.tensor_copy(key_scales[:], scale_pool[:, :T].indirect(offsets[:]))
+        q_codes, q_scales = quantize(q_grouped, "q")
+        load_vals("q_grouped")
+        key_codes = sbuf("key_codes", [P, I], U32)
         nc.vector.tensor_copy(key_codes[:], key_pool[:].indirect(offsets[:]))
-        bias_cols = listed_columns(bias_pool, BIAS_ROW, "bias", "key_pool")
-        val_pool3 = load_vals(3, "sharp_listed")
+        load_vals("key_pool")
+        sharp_cols = listed_columns(sharp_pool, SHARP_ROW, "sharp", None)
+        bias_cols = listed_columns(bias_pool, BIAS_ROW, "bias", None)
+        load_vals("bias_listed")
 
         size_rows = ps.tile([P, PACK, P], F32, tag="size")
         for t in range(PACK):
@@ -150,15 +140,23 @@ def tile_attend_tokensharpness_kernel(tc, query, keys_words, keys_scales, sharp,
             )
             nc.tensor.transpose(scores[:, r * P : (r + 1) * P], scores_t[:, r, :], ident[:])
 
-        v_grouped = [gather_vals(0, val_pool0, "bias_pool"), gather_vals(1, val_pool1)]
+        early_grouped = sbuf("early_grouped", [P, 4 * I], BF16)
+        v3_grouped = sbuf("v3_grouped", [P, I], BF16)
+        gather_vals(0, early_grouped[:, I : 2 * I], "raw", "bias_pool")
+        listed_vals1 = sbuf("listed_vals1", [P, I], BF16)
+        nc.vector.tensor_copy(listed_vals1[:], val_pools[1][:].indirect(offsets[:]))
 
-        neg_max = sbuf("neg_max", [P, 1], F32, "q_raw")
-        nc.vector.tensor_reduce(out=neg_max[:], in_=scores[:], axis=mybir.AxisListType.X, op=ALU.max, negate=True)
+        neg_scores = sbuf("neg_scores", [P, I], F32, "q_grouped")
+        neg_max = sbuf("neg_max", [P, 1], F32)
+        nc.vector.tensor_scalar(
+            out=neg_scores[:], in0=scores[:], scalar1=-1.0, scalar2=None, op0=ALU.mult, op1=ALU.min, accum_out=neg_max[:]
+        )
         probs = sbuf("probs", [P, I], F32)
         row_sum = sbuf("row_sum", [P, 1], F32)
         nc.scalar.activation(out=probs[:], in_=scores[:], func=ACT.Exp, bias=neg_max[:], accum_out=row_sum[:])
-        v_grouped.append(gather_vals(2, val_pool2))
-        inv_sum = sbuf("inv_sum", [P, 1], F32, "q_grouped")
+        turn(listed_vals1, early_grouped[:, 2 * I : 3 * I], "scores", "v1")
+        gather_vals(2, early_grouped[:, 3 * I :], "raw", "q_grouped")
+        inv_sum = sbuf("inv_sum", [P, 1], F32, "key_pool")
         nc.vector.reciprocal(inv_sum[:], row_sum[:])
         weights = sbuf("weights", [P, I], BF16)
         nc.vector.scalar_tensor_tensor(
@@ -169,26 +167,30 @@ def tile_attend_tokensharpness_kernel(tc, query, keys_words, keys_scales, sharp,
             op0=ALU.mult,
             op1=ALU.mult,
         )
-        w_grouped = turn(weights, "raw", "w")
-        v_grouped.append(gather_vals(3, val_pool3))
-        w_codes, w_scales = quantize(w_grouped, "w", "sharp_listed")
+        turn(weights, early_grouped[:, :I], "sharp", "w")
+        gather_vals(3, v3_grouped[:], "last", "probs")
+        early_codes, early_scales = quantize(early_grouped, "early", "bias_listed")
+        v3_codes, v3_scales = quantize(v3_grouped, "v3")
 
-        def product(blocks, bank_tag, copy):
-            acc = ps.tile([P, len(blocks), P], F32, tag=bank_tag, name=f"acc{blocks[0]}")
-            for n, j in enumerate(blocks):
-                v_codes, v_scales = quantize(v_grouped[j], f"v{j}")
-                nc.tensor.matmul_mx(
-                    out=acc[:, n, :],
-                    lhsT=w_codes[:].bitcast(FP8X4),
-                    lhsT_scale=w_scales[:],
-                    rhs=v_codes[:].bitcast(FP8X4),
-                    rhs_scale=v_scales[:],
-                    start=True,
-                    stop=True,
-                )
-            result = sbuf(f"result{blocks[0]}", [P, len(blocks) * P], F32)
-            copy(out=result[:], in_=acc[:].rearrange("q n e -> q (n e)"))
-            nc.sync.dma_start(out=out[:, blocks[0] * P : (blocks[-1] + 1) * P], in_=result[:])
+        def product(acc, codes, scales):
+            nc.tensor.matmul_mx(
+                out=acc,
+                lhsT=early_codes[:, :Q].bitcast(FP8X4),
+                lhsT_scale=early_scales[:, :Q],
+                rhs=codes.bitcast(FP8X4),
+                rhs_scale=scales,
+                start=True,
+                stop=True,
+            )
 
-        product([0, 1, 2], "sharp", nc.scalar.copy)
-        product([3], "bias", nc.vector.tensor_copy)
+        early = ps.tile([P, 3 * P], F32, tag="size")
+        product(early[:, : 2 * P], early_codes[:, Q : Q + 2 * P], early_scales[:, Q : Q + 2 * P])
+        product(early[:, 2 * P :], early_codes[:, Q + 2 * P :], early_scales[:, Q + 2 * P :])
+        early_out = sbuf("early_out", [P, 3 * P], F32)
+        nc.scalar.copy(out=early_out[:], in_=early[:])
+        nc.sync.dma_start(out=out[:, : 3 * P], in_=early_out[:])
+        late = ps.tile([P, P], F32, tag="bias")
+        product(late[:], v3_codes[:], v3_scales[:])
+        late_out = sbuf("late_out", [P, P], F32)
+        nc.vector.tensor_copy(out=late_out[:], in_=late[:])
+        nc.sync.dma_start(out=out[:, 3 * P :], in_=late_out[:])

from contextlib import ExitStack

import concourse.mybir as mybir
from concourse.masks import make_identity

D, T, I, Q, E = 512, 2048, 512, 128, 512
FLOPS = 2 * Q * I * (D + E)

F32 = mybir.dt.float32
BF16 = mybir.dt.bfloat16
I32 = mybir.dt.int32
U32 = mybir.dt.uint32
U16 = mybir.dt.uint16
U8 = mybir.dt.uint8
FP8X4 = mybir.dt.float8_e4m3fn_x4
ALU = mybir.AluOpType
ACT = mybir.ActivationFunctionType

P = 128
PACK = 4
SHARP_ROW = 8
BIAS_ROW = 72


def tile_attend_tokensharpness_kernel(tc, query, keys_words, keys_scales, sharp, tbias, size, vals, offs, out):
    nc = tc.nc
    with ExitStack() as ctx:
        sb = ctx.enter_context(tc.tile_pool(name="sb", bufs=1))
        ps = ctx.enter_context(tc.psum_pool(name="ps", bufs=1))

        def sbuf(name, shape, dtype, tag=None):
            return sb.tile(shape, dtype, align_bytes=64, name=name, tag=tag or name)

        def turn(pairs, grouped, bank_tag, name):
            words = pairs[:].bitcast(F32)
            turned = ps.tile([P, 2, P], F32, tag=bank_tag, name=name + "_turned")
            for u in range(2):
                nc.tensor.transpose(turned[:, u, :], words[:, u::2], ident[:])
            nc.scalar.copy(
                out=grouped.bitcast(F32).rearrange("p (c u) -> p c u", u=2),
                in_=turned[:].rearrange("p u c -> p c u"),
            )

        def quantize(grouped, name, tag=None):
            cols = grouped.shape[1] // PACK
            codes = sbuf(name + "_codes", [P, cols], U32, tag)
            scales = sbuf(name + "_scales", [P, cols], U8)
            nc.vector.quantize_mx(out=codes[:].bitcast(FP8X4), scales=scales[:], in_=grouped[:])
            return codes, scales

        def gather_vals(j, grouped, bank_tag, tag=None):
            listed = sbuf(f"listed_vals{j}", [P, I], BF16, tag)
            nc.vector.tensor_copy(listed[:], val_pools[j][:].indirect(offsets[:]))
            turn(listed, grouped, bank_tag, f"v{j}")

        def listed_columns(pool, row, name, tag):
            listed = sbuf(name + "_listed", [P, I], F32, tag)
            nc.vector.tensor_copy(listed[:], pool[:, :T].indirect(offsets[:]))
            turned = ps.tile([P, I // P, P], F32, tag=name, name=name + "_turned")
            for r in range(I // P):
                nc.tensor.transpose(turned[:, r, :], listed[:, r * P : (r + 1) * P], ident[:])
            cols = sbuf(name + "_cols", [P, I // P], F32)
            nc.scalar.activation(out=cols[:], in_=turned[:, :, row], func=ACT.Copy)
            return cols

        offsets = sb.tile([P, I // 16], U16)
        nc.sync.dma_start(offsets[:], offs)
        q_raw = sbuf("q_raw", [P, PACK, Q], F32)
        nc.sync.dma_start(out=q_raw[:], in_=query.rearrange("(p j) q -> p j q", j=PACK))
        size_cols = sbuf("size_cols", [P, PACK], F32)
        nc.sync.dma_start(out=size_cols[:], in_=size[0].rearrange("(p t) -> p t", t=PACK))
        scale_pool = sbuf("scale_pool", [P, T + 4], U8)
        nc.vector.memset(scale_pool[:].bitcast(I32), 0)
        for quad in range(4):
            nc.sync.dma_start(
                out=scale_pool[32 * quad : 32 * quad + 4, :T].bitcast(I32),
                in_=keys_scales[0, 4 * quad : 4 * quad + 4, :].bitcast(I32),
            )
        key_pool = sbuf("key_pool", [P, T], U32)
        nc.sync.dma_start(
            out=key_pool[:].bitcast(I32), in_=keys_words[0].rearrange("p n t -> p (n t)").bitcast(I32)
        )
        sharp_pool = sbuf("sharp_pool", [P, T + 1], F32)
        nc.vector.memset(sharp_pool[:].bitcast(I32), 0)
        nc.sync.dma_start(out=sharp_pool[SHARP_ROW : SHARP_ROW + 1, :T], in_=sharp[0:1, :])
        bias_pool = sbuf("bias_pool", [P, T], F32)
        nc.gpsimd.memset(bias_pool[:].bitcast(I32), 0)
        nc.sync.dma_start(out=bias_pool[BIAS_ROW : BIAS_ROW + 1, :], in_=tbias[0:1, :])
        ident = sbuf("ident", [P, P], F32)
        make_identity(nc, ident[:])
        val_pools = []

        def load_vals(tag):
            j = len(val_pools)
            val_pool = sbuf(f"val_pool{j}", [P, T], F32, tag)
            nc.sync.dma_start(out=val_pool[:], in_=vals[j * P : (j + 1) * P, :])
            val_pools.append(val_pool)

        q_grouped = sbuf("q_grouped", [P, Q * PACK], BF16)
        nc.scalar.copy(
            out=q_grouped[:].rearrange("p (q j) -> p q j", j=PACK), in_=q_raw[:].rearrange("p j q -> p q j")
        )
        load_vals("q_raw")
        key_scales = sbuf("key_scales", [P, I], U8)
        nc.vector.tensor_copy(key_scales[:], scale_pool[:, :T].indirect(offsets[:]))
        q_codes, q_scales = quantize(q_grouped, "q")
        load_vals("q_grouped")
        key_codes = sbuf("key_codes", [P, I], U32)
        nc.vector.tensor_copy(key_codes[:], key_pool[:].indirect(offsets[:]))
        load_vals("key_pool")
        sharp_cols = listed_columns(sharp_pool, SHARP_ROW, "sharp", None)
        bias_cols = listed_columns(bias_pool, BIAS_ROW, "bias", None)
        load_vals("bias_listed")

        size_rows = ps.tile([P, PACK, P], F32, tag="size")
        for t in range(PACK):
            nc.tensor.transpose(size_rows[:, t, :], size_cols[:, t : t + 1].to_broadcast([P, P]), ident[:])

        raw_scores = ps.tile([P, I // P, Q], F32, tag="raw")
        for r in range(I // P):
            slots = slice(r * P, (r + 1) * P)
            nc.tensor.matmul_mx(
                out=raw_scores[:, r, :],
                lhsT=key_codes[:, slots].bitcast(FP8X4),
                lhsT_scale=key_scales[:, slots],
                rhs=q_codes[:].bitcast(FP8X4),
                rhs_scale=q_scales[:],
                start=True,
                stop=True,
            )
        scores_t = sbuf("scores_t", [P, I // P, Q], F32)
        scores = ps.tile([P, I], F32, tag="scores")
        for r in range(I // P):
            nc.scalar.activation(
                out=scores_t[:, r, :],
                in_=raw_scores[:, r, :],
                func=ACT.Identity,
                scale=sharp_cols[:, r : r + 1],
                bias=bias_cols[:, r : r + 1],
            )
            nc.tensor.transpose(scores[:, r * P : (r + 1) * P], scores_t[:, r, :], ident[:])

        early_grouped = sbuf("early_grouped", [P, 4 * I], BF16)
        v3_grouped = sbuf("v3_grouped", [P, I], BF16)
        gather_vals(0, early_grouped[:, I : 2 * I], "raw", "bias_pool")
        listed_vals1 = sbuf("listed_vals1", [P, I], BF16)
        nc.vector.tensor_copy(listed_vals1[:], val_pools[1][:].indirect(offsets[:]))

        neg_scores = sbuf("neg_scores", [P, I], F32, "q_grouped")
        neg_max = sbuf("neg_max", [P, 1], F32)
        nc.vector.tensor_scalar(
            out=neg_scores[:], in0=scores[:], scalar1=-1.0, scalar2=None, op0=ALU.mult, op1=ALU.min, accum_out=neg_max[:]
        )
        probs = sbuf("probs", [P, I], F32)
        row_sum = sbuf("row_sum", [P, 1], F32)
        nc.scalar.activation(out=probs[:], in_=scores[:], func=ACT.Exp, bias=neg_max[:], accum_out=row_sum[:])
        turn(listed_vals1, early_grouped[:, 2 * I : 3 * I], "scores", "v1")
        gather_vals(2, early_grouped[:, 3 * I :], "raw", "q_grouped")
        inv_sum = sbuf("inv_sum", [P, 1], F32, "key_pool")
        nc.vector.reciprocal(inv_sum[:], row_sum[:])
        weights = sbuf("weights", [P, I], BF16)
        nc.vector.scalar_tensor_tensor(
            out=weights[:].rearrange("q (s t) -> q s t", t=PACK),
            in0=probs[:].rearrange("q (s t) -> q s t", t=PACK),
            scalar=inv_sum[:],
            in1=size_rows[:].rearrange("q t s -> q s t"),
            op0=ALU.mult,
            op1=ALU.mult,
        )
        turn(weights, early_grouped[:, :I], "sharp", "w")
        gather_vals(3, v3_grouped[:], "last", "probs")
        early_codes, early_scales = quantize(early_grouped, "early", "bias_listed")
        v3_codes, v3_scales = quantize(v3_grouped, "v3")

        def product(acc, codes, scales):
            nc.tensor.matmul_mx(
                out=acc,
                lhsT=early_codes[:, :Q].bitcast(FP8X4),
                lhsT_scale=early_scales[:, :Q],
                rhs=codes.bitcast(FP8X4),
                rhs_scale=scales,
                start=True,
                stop=True,
            )

        early = ps.tile([P, 3 * P], F32, tag="size")
        product(early[:, : 2 * P], early_codes[:, Q : Q + 2 * P], early_scales[:, Q : Q + 2 * P])
        product(early[:, 2 * P :], early_codes[:, Q + 2 * P :], early_scales[:, Q + 2 * P :])
        early_out = sbuf("early_out", [P, 3 * P], F32)
        nc.scalar.copy(out=early_out[:], in_=early[:])
        nc.sync.dma_start(out=out[:, : 3 * P], in_=early_out[:])
        late = ps.tile([P, P], F32, tag="bias")
        product(late[:], v3_codes[:], v3_scales[:])
        late_out = sbuf("late_out", [P, P], F32)
        nc.vector.tensor_copy(out=late_out[:], in_=late[:])
        nc.sync.dma_start(out=out[:, 3 * P :], in_=late_out[:])
